import numpy as np
import ml_dtypes


def mxq(x, axis, fmt="e4m3"):
    dtype, down = {"e4m3": (ml_dtypes.float8_e4m3fn, 7), "e5m2": (ml_dtypes.float8_e5m2, 14)}[fmt]
    v = np.moveaxis(np.asarray(x, np.float32).astype(ml_dtypes.bfloat16).astype(np.float64), axis, -1)
    blocks = v.reshape(v.shape[:-1] + (-1, 32))
    amax = np.abs(blocks).max(-1, keepdims=True)
    byte = np.maximum(np.where(amax > 0, np.frexp(amax)[1] - 1 + 127, 0) - down, 1)
    scale = np.exp2(byte - 127.0)
    codes = (blocks / scale).astype(np.float32).astype(dtype).astype(np.float64)
    return np.moveaxis((codes * scale).reshape(v.shape), -1, axis)


WIDE = False


def mx_kscale(k):
    if not WIDE:
        return np.ones(k)
    levels = np.array([10, -10, 5, -5, 0])
    if k % 512:
        return np.exp2(np.random.permutation(np.resize(levels, k // 32))).repeat(32)
    a = np.empty((k // 512, 16))
    for p in range(k // 512):
        a[p, :8] = np.random.permutation(np.resize(levels, 8))
        for g in range(8):
            far = levels[np.abs(levels - a[p, g]) >= 10]
            a[p, g + 8] = far[np.random.randint(len(far))]
    return np.exp2(a.ravel()).repeat(32)


def f64(x):
    return np.asarray(x).astype(np.float64)


def striped(idx):
    return np.tile(idx.reshape(-1, 16).T, (8, 1)).astype(np.uint16)


def unstriped(offs):
    return offs[:16].T.reshape(-1).astype(np.int64)


E2M1 = np.array([0.0, 0.5, 1.0, 1.5, 2.0, 3.0, 4.0, 6.0, -0.0, -0.5, -1.0, -1.5, -2.0, -3.0, -4.0, -6.0])


def pack_weight(w, fmt):
    k, n = w.shape
    w = f64(np.asarray(w, np.float32).astype(ml_dtypes.bfloat16)).reshape(k // 32, 32, n)
    amax = np.abs(w).max(1)
    if fmt == "e4m3":
        byte = np.frexp(amax)[1] - 1 + 127 - 7
    else:
        mant, ex = np.frexp(amax / 6.0)
        byte = np.where(mant > 0.5, ex, ex - 1) + 127
    byte = np.clip(np.where(amax > 0, byte, 1), 1, 254)
    scaled = (w * np.exp2(127.0 - byte)[:, None, :]).reshape(k, n).astype(np.float32)
    by_word = np.ascontiguousarray(scaled.reshape(k // 512, 128, 4, n).transpose(0, 1, 3, 2))
    if fmt == "e4m3":
        words = by_word.astype(ml_dtypes.float8_e4m3fn).view(np.uint8)
    else:
        c = by_word.astype(ml_dtypes.float4_e2m1fn).view(np.uint8) & 0xF
        words = (c[..., 0::2] | (c[..., 1::2] << 4)).reshape(k // 512, 128, 2 * n)
    return np.ascontiguousarray(words), np.ascontiguousarray(byte.astype(np.uint8).reshape(k // 512, 16, n))


def unpack_weight(words, scales, fmt):
    g, _, n = scales.shape
    words = np.ascontiguousarray(words).reshape(g, 128, n, -1)
    if fmt == "e4m3":
        vals = words.view(ml_dtypes.float8_e4m3fn).astype(np.float64)
    else:
        nib = np.empty((g, 128, n, 4), np.uint8)
        nib[..., 0::2] = words & 0xF
        nib[..., 1::2] = words >> 4
        vals = E2M1[nib]
    vals = vals * np.repeat(np.exp2(scales.astype(np.float64) - 127.0), 8, axis=1)[..., None]
    return vals.transpose(0, 1, 3, 2).reshape(g * 512, n)


def gelu(v):
    return 0.5 * v * (1.0 + np.tanh(np.sqrt(2.0 / np.pi) * (v + 0.044715 * v**3)))


K, KB, H, N, T, S, TB, P = 1024, 512, 1024, 512, 4096, 1024, 2048, 512

def setup_inputs():
    n = np.random.standard_normal
    s = mx_kscale(K)[:, None]
    s2 = mx_kscale(KB)[:, None]
    u = mx_kscale(H)[:, None]
    d = {}
    d["tab_words"], d["tab_scales"] = pack_weight(n((K, T)) * s, "e4m3")
    d["tab2_words"], d["tab2_scales"] = pack_weight(n((KB, TB)) * s2, "e4m3")
    d["offs"] = striped(np.random.permutation(T)[:S])
    d["offs2"] = striped(np.random.permutation(TB)[:P])
    d["pos1"] = striped(np.random.permutation(S)[:P])
    d["wa_words"], d["wa_scales"] = pack_weight(n((K, H)) / K**0.5 / s * u.T, "e2m1")
    d["wb"] = (1.8 * n((KB, H)) / KB**0.5 / s2).astype(np.float32)
    d["gb"] = (1.3 * np.exp(0.3 * n(H)) * u[:, 0]).astype(np.float32)
    d["wgs"] = np.exp(0.3 * n((128, P))).astype(np.float32)
    d["gz"] = (0.7 * np.exp(0.3 * n(H)) / u[:, 0]).astype(np.float32)
    d["wz"] = (n((H, N)) / H**0.5 / u).astype(np.float32)
    d["wk_words"], d["wk_scales"] = pack_weight(n((H, N)) / H**0.5 / u, "e4m3")
    return d

def reference(tab_words, tab_scales, tab2_words, tab2_scales, offs, offs2, pos1,
              wa_words, wa_scales, wb, gb, wgs, gz, wz, wk_words, wk_scales):
    v = unpack_weight(tab_words, tab_scales, "e4m3")[:, unstriped(offs)]
    v2 = unpack_weight(tab2_words, tab2_scales, "e4m3")[:, unstriped(offs2)]
    wa = unpack_weight(wa_words, wa_scales, "e2m1")
    wk = unpack_weight(wk_words, wk_scales, "e4m3")
    a = wa.T @ v
    b = np.tanh(mxq(f64(wb), 0, "e4m3").T @ v2) * f64(gb)[:, None]
    placed = np.zeros((H, S))
    placed[:, unstriped(pos1)] = np.tile(f64(wgs), (H // 128, 1)) * b
    z = np.square(a - placed) * f64(gz)[:, None]
    zq = mxq(z, 0, "e4m3")
    aq = mxq(a, 0, "e4m3")
    return mxq(f64(wz), 0, "e4m3").T @ zq + wk.T @ aq

@@ -1,0 +1,261 @@
+from contextlib import ExitStack
+
+import concourse.mybir as mybir
+
+K, KB, H, N, T, S, TB, PL = 1024, 512, 1024, 512, 4096, 1024, 2048, 512
+FLOPS = 2 * K * H * S + 2 * KB * H * PL + 2 * 2 * H * N * S
+
+F32 = mybir.dt.float32
+BF16 = mybir.dt.bfloat16
+I32 = mybir.dt.int32
+U32 = mybir.dt.uint32
+U16 = mybir.dt.uint16
+U8 = mybir.dt.uint8
+FP8X4 = mybir.dt.float8_e4m3fn_x4
+FP4X4 = mybir.dt.float4_e2m1fn_x4
+ALU = mybir.AluOpType
+ACT = mybir.ActivationFunctionType
+
+P = 128
+CH = 128
+QW = 256
+A_BANKS = 6
+
+
+def tile_list_ballot_audit_disagreement_kernel(
+    tc, tab_words, tab_scales, tab2_words, tab2_scales, offs, offs2, pos1,
+    wa_words, wa_scales, wb, gb, wgs, gz, wz, wk_words, wk_scales, out,
+):
+    nc = tc.nc
+    with ExitStack() as ctx:
+        lists = ctx.enter_context(tc.tile_pool(name="lists", bufs=1))
+        keep = ctx.enter_context(tc.tile_pool(name="keep", bufs=1))
+        ring = ctx.enter_context(tc.tile_pool(name="ring", bufs=2))
+        psum = ctx.enter_context(tc.psum_pool(name="psum", bufs=1))
+
+        offs_t = lists.tile([P, S // 16], U16, name="offs_t")
+        offs2_t = lists.tile([P, PL // 16], U16, name="offs2_t")
+        pos_t = lists.tile([P, PL // 16], U16, name="pos_t")
+
+        def held(shape, dtype, name, tag=""):
+            return keep.tile(shape, dtype, name=name, tag=tag, align_bytes=64)
+
+        tab2_w = held([P, TB], U32, "tab2_w", "slot_a")
+        tab2_s = held([P, TB], U8, "tab2_s", "slot_b")
+        tab_w = [held([P, T], U32, "tab_w0", "slot_c")]
+        tab_s = held([P, T], U8, "tab_s")
+        wa_raw = held([P, 2, H], U16, "wa_raw", "slot_d")
+        wa_w = held([P, 2, H], U16, "wa_w")
+        wa_sraw = held([P, 2, H], U8, "wa_sraw")
+        wa_s = held([P, 2, H], U8, "wa_s")
+        wk_s = held([P, 2, N], U8, "wk_s")
+        wgs_t = [held([P, 2, PL], F32, "wgs_t0")]
+        pages = [held([P, S], F32, "page%d" % t) for t in range(4)]
+        v_w = [held([P, S], U32, "v_w%d" % a) for a in range(2)]
+        v_s = [held([P, S], U8, "v_s%d" % a) for a in range(2)]
+        v2_w = held([P, PL], U32, "v2_w")
+        v2_s = held([P, PL], U8, "v2_s")
+        gz_t = held([P, 8], F32, "gz_t")
+        gb_t = held([P, 8], F32, "gb_t")
+
+        nc.vector.memset(tab_s[:].bitcast(I32), 0)
+        nc.vector.memset(wa_sraw[:].bitcast(I32), 0)
+        nc.vector.memset(wk_s[:].bitcast(I32), 0)
+        nc.vector.memset(v_s[1][:].bitcast(I32), 0)
+        for t in range(4):
+            nc.vector.memset(pages[t][:], 0.0)
+
+        nc.sync.dma_start(out=gz_t[:].rearrange("p (b t) -> p b t", b=2), in_=gz.rearrange("(b p t) -> p b t", b=2, t=4))
+        nc.scalar.dma_start(out=gb_t[:].rearrange("p (b t) -> p b t", b=2), in_=gb.rearrange("(b p t) -> p b t", b=2, t=4))
+        nc.sync.dma_start(offs2_t[:], offs2)
+        for q in range(4):
+            rows = tab2_scales[0, 4 * q : 4 * q + 4, :].bitcast(I32).unsqueeze(0).to_broadcast([8, 4, TB // 4])
+            nc.scalar.dma_start(out=tab2_s[32 * q : 32 * q + 32, :].bitcast(I32), in_=rows)
+        nc.sync.dma_start(out=tab2_w[:].bitcast(I32), in_=tab2_words[0].rearrange("p t i -> p (t i)").bitcast(I32))
+
+        def load_rows(src, name, tag):
+            raw = held([P, 4, 512], F32, name, tag)
+            nc.sync.dma_start(out=raw[:], in_=src.rearrange("(p j) c -> p j c", j=4))
+            return raw
+
+        def load_wgs(h):
+            rows = wgs.rearrange("(q t) c -> q t c", t=4)[:, 2 * h : 2 * h + 2, :]
+            for q in range(4):
+                nc.sync.dma_start(out=wgs_t[h][32 * q : 32 * q + 32, :, :], in_=rows)
+
+        def load_table(a):
+            nc.sync.dma_start(out=tab_w[a][:].bitcast(I32), in_=tab_words[a].rearrange("p t i -> p (t i)").bitcast(I32))
+
+        def load_planes(dst, src):
+            rows = src.rearrange("a (q r) c -> r q a c", r=4)
+            for r in range(4):
+                nc.sync.dma_start(out=dst[r:P:32, :, :].bitcast(I32), in_=rows[r].bitcast(I32))
+
+        wb_raw = [load_rows(wb[:, 0:512], "wb_raw0", "slot_e")]
+        nc.sync.dma_start(pos_t[:], pos1)
+        load_wgs(0)
+        load_table(0)
+        nc.sync.dma_start(offs_t[:], offs)
+        for q in range(4):
+            nc.sync.dma_start(out=tab_s[32 * q : 32 * q + 8, :].bitcast(I32), in_=tab_scales[:, 4 * q : 4 * q + 4, :].bitcast(I32))
+        nc.sync.dma_start(out=wa_raw[:].bitcast(I32), in_=wa_words.rearrange("a p c -> p a c").bitcast(I32))
+        load_planes(wa_sraw, wa_scales)
+        load_planes(wk_s, wk_scales)
+
+        def small(name):
+            return held([P, 8], F32, name)
+
+        twice, sign, mag, safe = small("twice"), small("sign"), small("mag"), small("safe")
+        guess, inverse, ratio = small("guess"), small("inverse"), small("ratio")
+        root, root_gb = small("root"), small("root_gb")
+        nc.vector.scalar_tensor_tensor(mag[:], gz_t[:], -1.0, gz_t[:], ALU.mult, ALU.max)
+        nc.vector.tensor_scalar(safe[:], mag[:], 1e-30, None, ALU.max)
+        nc.scalar.activation(guess[:], safe[:], ACT.Sqrt)
+        warm = held([P, 8], F32, "warm")
+        nc.scalar.activation(warm[:], guess[:], ACT.Tanh)
+        nc.vector.reciprocal(inverse[:], guess[:])
+        nc.vector.tensor_tensor(ratio[:], mag[:], inverse[:], ALU.mult)
+        nc.vector.tensor_tensor(root[:], ratio[:], guess[:], ALU.add)
+        nc.vector.tensor_tensor(root_gb[:], root[:], gb_t[:], ALU.mult)
+        nc.vector.tensor_scalar(twice[:], gz_t[:], 0.0, 2.0, ALU.is_ge, ALU.mult)
+        nc.vector.tensor_scalar(sign[:], twice[:], -1.0, None, ALU.add)
+
+        nc.vector.tensor_copy(v2_w[:], tab2_w[:].indirect(offs2_t[:]))
+        nc.vector.tensor_copy(v2_s[:], tab2_s[:].indirect(offs2_t[:]))
+        tab_w.append(held([P, T], U32, "tab_w1", "slot_a"))
+        load_table(1)
+        wb_raw.append(load_rows(wb[:, 512:1024], "wb_raw1", "slot_b"))
+
+        def quantize(src, width, name):
+            codes = held([P, width], U32, name + "_w")
+            scales = held([P, width], U8, name + "_s")
+            nc.vector.quantize_mx(out=codes[:].bitcast(FP8X4), scales=scales[:], in_=src)
+            return codes, scales
+
+        def cast_wb(b):
+            grouped = ring.tile([P, 4, P, 4], BF16, name="wb_bf%d" % b, tag="grouped", align_bytes=64)
+            dst = grouped[:].rearrange("p t m j -> p m j t")
+            src = wb_raw[b][:].rearrange("p j (m t) -> p m j t", t=4)
+            if b == 0:
+                nc.vector.tensor_copy(dst[:, 0:64], src[:, 0:64])
+                nc.scalar.copy(dst[:, 64:128], src[:, 64:128])
+            else:
+                nc.scalar.copy(dst, src)
+            return grouped
+
+        def place(b, t, grouped):
+            codes, scales = quantize(grouped[:, t].rearrange("p m j -> p (m j)"), P, "wb%d%d" % (b, t))
+            bank = psum.tile([P, PL], F32, name="b_bank", tag="bo", bufs=2)
+            nc.tensor.matmul_mx(out=bank[:], lhsT=codes[:].bitcast(FP8X4), lhsT_scale=scales[:],
+                                rhs=v2_w[:].bitcast(FP8X4), rhs_scale=v2_s[:], start=True, stop=True)
+            weight = ring.tile([P, PL], F32, name="weight", bufs=8)
+            nc.scalar.activation(weight[:], wgs_t[t // 2][:, t % 2, :], ACT.Copy, scale=root_gb[:, 4 * b + t : 4 * b + t + 1])
+            hand = ring.tile([P, PL], F32, name="hand", bufs=8)
+            nc.scalar.activation(hand[:], bank[:], ACT.Tanh)
+            nc.vector.tensor_tensor(pages[t][:].indirect(pos_t[:]), hand[:], weight[:], ALU.mult)
+
+        grouped0 = cast_wb(0)
+        wgs_t.append(held([P, 2, PL], F32, "wgs_t1", "slot_e"))
+        load_wgs(1)
+        place(0, 0, grouped0)
+        place(0, 1, grouped0)
+
+        nc.vector.tensor_copy(v_s[0][:], tab_s[:].indirect(offs_t[:]))
+        for q in range(4):
+            nc.sync.dma_start(out=v_s[1][32 * q : 32 * q + 4, :].bitcast(I32), in_=v_s[0][32 * q + 4 : 32 * q + 8, :].bitcast(I32))
+        nc.vector.tensor_copy(v_w[0][:], tab_w[0][:].indirect(offs_t[:]))
+        wz_raw = held([P, 2, 4, N], F32, "wz_raw", "slot_c")
+        for b in range(2):
+            nc.sync.dma_start(out=wz_raw[:, b], in_=wz[512 * b : 512 * b + 512, :].rearrange("(p j) c -> p j c", j=4))
+        for dealt, raw in ((wa_w, wa_raw), (wa_s, wa_sraw)):
+            nc.vector.tensor_copy(dealt[:].rearrange("p a (b t m) -> p (a b) m t", b=2, t=4),
+                                  raw[:].rearrange("p a (b m t) -> p (a b) m t", b=2, t=4))
+        wk_w = held([P, 2, N], U32, "wk_w", "slot_d")
+        nc.sync.dma_start(out=wk_w[:].bitcast(I32), in_=wk_words.rearrange("a p c i -> p a (c i)").bitcast(I32))
+        nc.vector.tensor_copy(v_w[1][:], tab_w[1][:].indirect(offs_t[:]))
+        place(0, 2, grouped0)
+        place(0, 3, grouped0)
+        grouped1 = cast_wb(1)
+
+        def quantize_wz(b):
+            signed = ring.tile([P, 4, N], BF16, name="signed", bufs=1)
+            for j in range(4):
+                nc.scalar.activation(signed[:, j, :], wz_raw[:, b, j, :], ACT.Copy, scale=sign[:, 4 * b + j : 4 * b + j + 1])
+            grouped = ring.tile([P, 4, P, 4], BF16, name="wz_bf%d" % b, tag="grouped", align_bytes=64)
+            nc.scalar.copy(grouped[:].rearrange("p s (c i) j -> p (s c) j i", i=4), signed[:].rearrange("p j (c i) -> p c j i", i=4))
+            return quantize(grouped[:].rearrange("p s m j -> p (s m j)"), N, "wz%d" % b)
+
+        def machine(b, c, a_bf):
+            bank = psum.tile([P, 4, CH], F32, name="a_bank", tag="a", bufs=A_BANKS)
+            cols = slice(CH * c, CH * c + CH)
+            for a in range(2):
+                for t in range(4):
+                    rows = slice(512 * b + P * t, 512 * b + P * t + P)
+                    nc.tensor.matmul_mx(out=bank[:, t, :], lhsT=wa_w[:, a, rows].bitcast(FP4X4), lhsT_scale=wa_s[:, a, rows],
+                                        rhs=v_w[a][:, cols].bitcast(FP8X4), rhs_scale=v_s[a][:, cols],
+                                        start=(a == 0 and t == 0), stop=(a == 1 and t == 3))
+            half = c % 2
+            nc.scalar.copy(a_bf[:, CH * half : CH * half + CH, :], bank[:].rearrange("p t c -> p c t"))
+            diff = ring.tile([P, 4, CH], F32, name="diff", bufs=8)
+            for t in range(4):
+                nc.vector.scalar_tensor_tensor(diff[:, t, :], bank[:, t, :], root[:, 4 * b + t : 4 * b + t + 1],
+                                               pages[t][:, cols], ALU.mult, ALU.subtract)
+            return diff
+
+        def square(c, diff, z_bf):
+            half = c % 2
+            nc.scalar.activation(z_bf[:, CH * half : CH * half + CH, :].rearrange("p (c i) t -> p c t i", i=4),
+                                 diff[:].rearrange("p t (c i) -> p c t i", i=4), ACT.Square, scale=0.5)
+
+        aq, zq = {}, {}
+
+        def quantize_tile(src, name):
+            return quantize(src[:].rearrange("p c t -> p (c t)"), QW, name)
+
+        def read_out(q, wzq):
+            for k in range(2):
+                if q % 3 == 0:
+                    bank = psum.tile([P, 2, QW], F32, name="o_bank", tag="bo", bufs=2)
+                else:
+                    bank = psum.tile([P, 2, QW], F32, name="o_bank", tag="a", bufs=A_BANKS)
+                passes = [((wk_w[:, b], wk_s[:, b]), aq[b, q]) for b in range(2)]
+                passes = passes + [((wzq[b][0][:], wzq[b][1][:]), zq[b, q]) for b in range(2)]
+                for i, (weights, moving) in enumerate(passes):
+                    for s in range(2):
+                        cols = slice(P * (2 * k + s), P * (2 * k + s) + P)
+                        nc.tensor.matmul_mx(out=bank[:, s, :], lhsT=weights[0][:, cols].bitcast(FP8X4), lhsT_scale=weights[1][:, cols],
+                                            rhs=moving[0][:].bitcast(FP8X4), rhs_scale=moving[1][:],
+                                            start=(i == 0 and s == 0), stop=(i == 3 and s == 1))
+                staged = ring.tile([P, 2, QW], F32, name="staged", bufs=4)
+                if k == 0:
+                    nc.vector.tensor_copy(staged[:], bank[:])
+                else:
+                    nc.scalar.copy(staged[:], bank[:])
+                nc.sync.dma_start(
+                    out=out[2 * P * k : 2 * P * k + 2 * P, QW * q : QW * q + QW].rearrange("(s p) j -> p s j", s=2), in_=staged[:])
+
+        diffs = []
+        for q in range(4):
+            a_bf = ring.tile([P, QW, 4], BF16, name="a_bf", bufs=4, align_bytes=64)
+            diffs.extend(machine(0, 2 * q + h, a_bf) for h in range(2))
+            aq[0, q] = quantize_tile(a_bf, "a0%d" % q)
+        for t in range(4):
+            place(1, t, grouped1)
+        for q in range(4):
+            z_bf = ring.tile([P, QW, 4], BF16, name="z_bf", bufs=4, align_bytes=64)
+            for h in range(2):
+                square(2 * q + h, diffs[2 * q + h], z_bf)
+            zq[0, q] = quantize_tile(z_bf, "z0%d" % q)
+        wzq = [quantize_wz(b) for b in range(2)]
+
+        for q in range(4):
+            a_bf = ring.tile([P, QW, 4], BF16, name="a_bf", bufs=4, align_bytes=64)
+            pair = [machine(1, 2 * q + h, a_bf) for h in range(2)]
+            aq[1, q] = quantize_tile(a_bf, "a1%d" % q)
+            z_bf = ring.tile([P, QW, 4], BF16, name="z_bf", bufs=4, align_bytes=64)
+            for h in range(2):
+                square(2 * q + h, pair[h], z_bf)
+            zq[1, q] = quantize_tile(z_bf, "z1%d" % q)
+            if q > 0:
+                read_out(q - 1, wzq)
+        read_out(3, wzq)

@@ -46,8 +46,8 @@ def tile_list_ballot_audit_disagreement_kernel(
         tab_s = held([P, T], U8, "tab_s")
         wa_raw = held([P, 2, H], U16, "wa_raw", "slot_d")
         wa_w = held([P, 2, H], U16, "wa_w")
-        wa_sraw = held([P, 2, H], U8, "wa_sraw")
-        wa_s = held([P, 2, H], U8, "wa_s")
+        wa_sraw = held([P, H], U8, "wa_sraw")
+        wa_s = [held([P, H], U8, "wa_s%d" % a) for a in range(2)]
         wk_s = held([P, 2, N], U8, "wk_s")
         wgs_t = [held([P, 2, PL], F32, "wgs_t0")]
         pages = [held([P, S], F32, "page%d" % t) for t in range(4)]
@@ -58,19 +58,20 @@ def tile_list_ballot_audit_disagreement_kernel(
         gz_t = held([P, 8], F32, "gz_t")
         gb_t = held([P, 8], F32, "gb_t")
 
-        nc.vector.memset(tab_s[:].bitcast(I32), 0)
-        nc.vector.memset(wa_sraw[:].bitcast(I32), 0)
-        nc.vector.memset(wk_s[:].bitcast(I32), 0)
-        nc.vector.memset(v_s[1][:].bitcast(I32), 0)
+        nc.gpsimd.memset(tab_s[:].bitcast(I32), 0)
+        nc.gpsimd.memset(wa_sraw[:].bitcast(I32), 0)
+        nc.gpsimd.memset(wk_s[:].bitcast(I32), 0)
+        nc.gpsimd.memset(v_s[1][:].bitcast(I32), 0)
+        nc.gpsimd.memset(wa_s[1][:].bitcast(I32), 0)
         for t in range(4):
             nc.vector.memset(pages[t][:], 0.0)
 
         nc.sync.dma_start(out=gz_t[:].rearrange("p (b t) -> p b t", b=2), in_=gz.rearrange("(b p t) -> p b t", b=2, t=4))
-        nc.scalar.dma_start(out=gb_t[:].rearrange("p (b t) -> p b t", b=2), in_=gb.rearrange("(b p t) -> p b t", b=2, t=4))
+        nc.sync.dma_start(out=gb_t[:].rearrange("p (b t) -> p b t", b=2), in_=gb.rearrange("(b p t) -> p b t", b=2, t=4))
         nc.sync.dma_start(offs2_t[:], offs2)
         for q in range(4):
             rows = tab2_scales[0, 4 * q : 4 * q + 4, :].bitcast(I32).unsqueeze(0).to_broadcast([8, 4, TB // 4])
-            nc.scalar.dma_start(out=tab2_s[32 * q : 32 * q + 32, :].bitcast(I32), in_=rows)
+            nc.sync.dma_start(out=tab2_s[32 * q : 32 * q + 32, :].bitcast(I32), in_=rows)
         nc.sync.dma_start(out=tab2_w[:].bitcast(I32), in_=tab2_words[0].rearrange("p t i -> p (t i)").bitcast(I32))
 
         def load_rows(src, name, tag):
@@ -91,15 +92,22 @@ def tile_list_ballot_audit_disagreement_kernel(
             for r in range(4):
                 nc.sync.dma_start(out=dst[r:P:32, :, :].bitcast(I32), in_=rows[r].bitcast(I32))
 
+        def load_packed(dst, src):
+            for q in range(4):
+                nc.sync.dma_start(out=dst[32 * q : 32 * q + 8, :].bitcast(I32), in_=src[:, 4 * q : 4 * q + 4, :].bitcast(I32))
+
+        def lift_second_plane(planes):
+            for q in range(4):
+                nc.sync.dma_start(out=planes[1][32 * q : 32 * q + 4, :].bitcast(I32), in_=planes[0][32 * q + 4 : 32 * q + 8, :].bitcast(I32))
+
         wb_raw = [load_rows(wb[:, 0:512], "wb_raw0", "slot_e")]
         nc.sync.dma_start(pos_t[:], pos1)
         load_wgs(0)
         load_table(0)
         nc.sync.dma_start(offs_t[:], offs)
-        for q in range(4):
-            nc.sync.dma_start(out=tab_s[32 * q : 32 * q + 8, :].bitcast(I32), in_=tab_scales[:, 4 * q : 4 * q + 4, :].bitcast(I32))
+        load_packed(tab_s, tab_scales)
         nc.sync.dma_start(out=wa_raw[:].bitcast(I32), in_=wa_words.rearrange("a p c -> p a c").bitcast(I32))
-        load_planes(wa_sraw, wa_scales)
+        load_packed(wa_sraw, wa_scales)
         load_planes(wk_s, wk_scales)
 
         def small(name):
@@ -122,18 +130,21 @@ def tile_list_ballot_audit_disagreement_kernel(
 
         nc.vector.tensor_copy(v2_w[:], tab2_w[:].indirect(offs2_t[:]))
         nc.vector.tensor_copy(v2_s[:], tab2_s[:].indirect(offs2_t[:]))
-        tab_w.append(held([P, T], U32, "tab_w1", "slot_a"))
+        wz_raw = held([P, 2, 4, N], F32, "wz_raw", "slot_a")
+        for b in range(2):
+            nc.sync.dma_start(out=wz_raw[:, b], in_=wz[512 * b : 512 * b + 512, :].rearrange("(p j) c -> p j c", j=4))
+        tab_w.append(held([P, T], U32, "tab_w1", "slot_b"))
         load_table(1)
-        wb_raw.append(load_rows(wb[:, 512:1024], "wb_raw1", "slot_b"))
 
-        def quantize(src, width, name):
-            codes = held([P, width], U32, name + "_w")
+        def quantize(src, width, name, codes=None):
+            if codes is None:
+                codes = held([P, width], U32, name + "_w")
             scales = held([P, width], U8, name + "_s")
             nc.vector.quantize_mx(out=codes[:].bitcast(FP8X4), scales=scales[:], in_=src)
             return codes, scales
 
         def cast_wb(b):
-            grouped = ring.tile([P, 4, P, 4], BF16, name="wb_bf%d" % b, tag="grouped", align_bytes=64)
+            grouped = ring.tile([P, 4, P, 4], BF16, name="wb_bf%d" % b, tag="grouped", bufs=3, align_bytes=64)
             dst = grouped[:].rearrange("p t m j -> p m j t")
             src = wb_raw[b][:].rearrange("p j (m t) -> p m j t", t=4)
             if b == 0:
@@ -143,47 +154,59 @@ def tile_list_ballot_audit_disagreement_kernel(
                 nc.scalar.copy(dst, src)
             return grouped
 
-        def place(b, t, grouped):
-            codes, scales = quantize(grouped[:, t].rearrange("p m j -> p (m j)"), P, "wb%d%d" % (b, t))
+        def quantize_wb(grouped, t0, t1, name):
+            codes, scales = quantize(grouped[:, t0:t1].rearrange("p t m j -> p (t m j)"), P * (t1 - t0), name)
+            return [(codes[:, P * i : P * i + P], scales[:, P * i : P * i + P]) for i in range(t1 - t0)]
+
+        def place(b, t, weights):
+            codes, scales = weights[t]
             bank = psum.tile([P, PL], F32, name="b_bank", tag="bo", bufs=2)
-            nc.tensor.matmul_mx(out=bank[:], lhsT=codes[:].bitcast(FP8X4), lhsT_scale=scales[:],
+            nc.tensor.matmul_mx(out=bank[:], lhsT=codes.bitcast(FP8X4), lhsT_scale=scales,
                                 rhs=v2_w[:].bitcast(FP8X4), rhs_scale=v2_s[:], start=True, stop=True)
-            weight = ring.tile([P, PL], F32, name="weight", bufs=8)
+            if (b, t) == (1, 3):
+                weight = held([P, PL], F32, "weight_last", "slot_f0")
+            else:
+                weight = ring.tile([P, PL], F32, name="weight", bufs=7)
             nc.scalar.activation(weight[:], wgs_t[t // 2][:, t % 2, :], ACT.Copy, scale=root_gb[:, 4 * b + t : 4 * b + t + 1])
-            hand = ring.tile([P, PL], F32, name="hand", bufs=8)
+            if (b, t) == (1, 3):
+                hand = held([P, PL], F32, "hand_last", "slot_g")
+            else:
+                hand = ring.tile([P, PL], F32, name="hand", bufs=7)
             nc.scalar.activation(hand[:], bank[:], ACT.Tanh)
             nc.vector.tensor_tensor(pages[t][:].indirect(pos_t[:]), hand[:], weight[:], ALU.mult)
 
         grouped0 = cast_wb(0)
         wgs_t.append(held([P, 2, PL], F32, "wgs_t1", "slot_e"))
         load_wgs(1)
-        place(0, 0, grouped0)
-        place(0, 1, grouped0)
+        wbq0 = quantize_wb(grouped0, 0, 1, "wb00")
+        place(0, 0, wbq0)
+        wbq0 = wbq0 + quantize_wb(grouped0, 1, 2, "wb01") + quantize_wb(grouped0, 2, 4, "wb02")
+        place(0, 1, wbq0)
 
         nc.vector.tensor_copy(v_s[0][:], tab_s[:].indirect(offs_t[:]))
-        for q in range(4):
-            nc.sync.dma_start(out=v_s[1][32 * q : 32 * q + 4, :].bitcast(I32), in_=v_s[0][32 * q + 4 : 32 * q + 8, :].bitcast(I32))
+        lift_second_plane(v_s)
+        nc.vector.tensor_copy(wa_s[0][:].rearrange("p (b t m) -> p b m t", b=2, t=4), wa_sraw[:].rearrange("p (b m t) -> p b m t", b=2, t=4))
+        lift_second_plane(wa_s)
         nc.vector.tensor_copy(v_w[0][:], tab_w[0][:].indirect(offs_t[:]))
-        wz_raw = held([P, 2, 4, N], F32, "wz_raw", "slot_c")
-        for b in range(2):
-            nc.sync.dma_start(out=wz_raw[:, b], in_=wz[512 * b : 512 * b + 512, :].rearrange("(p j) c -> p j c", j=4))
-        for dealt, raw in ((wa_w, wa_raw), (wa_s, wa_sraw)):
-            nc.vector.tensor_copy(dealt[:].rearrange("p a (b t m) -> p (a b) m t", b=2, t=4),
-                                  raw[:].rearrange("p a (b m t) -> p (a b) m t", b=2, t=4))
+        wb_raw.append(load_rows(wb[:, 512:1024], "wb_raw1", "slot_c"))
+        nc.vector.tensor_copy(wa_w[:].rearrange("p a (b t m) -> p (a b) m t", b=2, t=4),
+                              wa_raw[:].rearrange("p a (b m t) -> p (a b) m t", b=2, t=4))
         wk_w = held([P, 2, N], U32, "wk_w", "slot_d")
         nc.sync.dma_start(out=wk_w[:].bitcast(I32), in_=wk_words.rearrange("a p c i -> p a (c i)").bitcast(I32))
         nc.vector.tensor_copy(v_w[1][:], tab_w[1][:].indirect(offs_t[:]))
-        place(0, 2, grouped0)
-        place(0, 3, grouped0)
-        grouped1 = cast_wb(1)
 
         def quantize_wz(b):
             signed = ring.tile([P, 4, N], BF16, name="signed", bufs=1)
             for j in range(4):
                 nc.scalar.activation(signed[:, j, :], wz_raw[:, b, j, :], ACT.Copy, scale=sign[:, 4 * b + j : 4 * b + j + 1])
-            grouped = ring.tile([P, 4, P, 4], BF16, name="wz_bf%d" % b, tag="grouped", align_bytes=64)
+            grouped = ring.tile([P, 4, P, 4], BF16, name="wz_bf%d" % b, tag="grouped", bufs=3, align_bytes=64)
             nc.scalar.copy(grouped[:].rearrange("p s (c i) j -> p (s c) j i", i=4), signed[:].rearrange("p j (c i) -> p c j i", i=4))
             return quantize(grouped[:].rearrange("p s m j -> p (s m j)"), N, "wz%d" % b)
+
+        wzq = [quantize_wz(b) for b in range(2)]
+        place(0, 2, wbq0)
+        place(0, 3, wbq0)
+        wbq1 = quantize_wb(cast_wb(1), 0, 4, "wb1")
 
         def machine(b, c, a_bf):
             bank = psum.tile([P, 4, CH], F32, name="a_bank", tag="a", bufs=A_BANKS)
@@ -191,71 +214,93 @@ def tile_list_ballot_audit_disagreement_kernel(
             for a in range(2):
                 for t in range(4):
                     rows = slice(512 * b + P * t, 512 * b + P * t + P)
-                    nc.tensor.matmul_mx(out=bank[:, t, :], lhsT=wa_w[:, a, rows].bitcast(FP4X4), lhsT_scale=wa_s[:, a, rows],
+                    nc.tensor.matmul_mx(out=bank[:, t, :], lhsT=wa_w[:, a, rows].bitcast(FP4X4), lhsT_scale=wa_s[a][:, rows],
                                         rhs=v_w[a][:, cols].bitcast(FP8X4), rhs_scale=v_s[a][:, cols],
                                         start=(a == 0 and t == 0), stop=(a == 1 and t == 3))
-            half = c % 2
-            nc.scalar.copy(a_bf[:, CH * half : CH * half + CH, :], bank[:].rearrange("p t c -> p c t"))
-            diff = ring.tile([P, 4, CH], F32, name="diff", bufs=8)
-            for t in range(4):
-                nc.vector.scalar_tensor_tensor(diff[:, t, :], bank[:, t, :], root[:, 4 * b + t : 4 * b + t + 1],
-                                               pages[t][:, cols], ALU.mult, ALU.subtract)
-            return diff
+            part = c % 4
+            nc.scalar.copy(a_bf[:, CH * part : CH * part + CH, :], bank[:].rearrange("p t c -> p c t"))
+            return bank
 
-        def square(c, diff, z_bf):
-            half = c % 2
-            nc.scalar.activation(z_bf[:, CH * half : CH * half + CH, :].rearrange("p (c i) t -> p c t i", i=4),
-                                 diff[:].rearrange("p t (c i) -> p c t i", i=4), ACT.Square, scale=0.5)
+        def subtract(b, t, dst, src, cols):
+            nc.vector.scalar_tensor_tensor(dst, src, root[:, 4 * b + t : 4 * b + t + 1], pages[t][:, cols], ALU.mult, ALU.subtract)
 
-        aq, zq = {}, {}
+        def square(dst, src):
+            nc.scalar.activation(dst.rearrange("p (c i) t -> p c t i", i=4), src.rearrange("p t (c i) -> p c t i", i=4),
+                                 ACT.Square, scale=0.5)
 
-        def quantize_tile(src, name):
-            return quantize(src[:].rearrange("p c t -> p (c t)"), QW, name)
+        def quantize_tokens(src, width, name, codes=None):
+            codes, scales = quantize(src.rearrange("p c t -> p (c t)"), width, name, codes)
+            return [(codes[:, QW * i : QW * i + QW], scales[:, QW * i : QW * i + QW]) for i in range(width // QW)]
 
-        def read_out(q, wzq):
+        def read_out(q):
             for k in range(2):
-                if q % 3 == 0:
+                if q == 0:
                     bank = psum.tile([P, 2, QW], F32, name="o_bank", tag="bo", bufs=2)
                 else:
                     bank = psum.tile([P, 2, QW], F32, name="o_bank", tag="a", bufs=A_BANKS)
-                passes = [((wk_w[:, b], wk_s[:, b]), aq[b, q]) for b in range(2)]
-                passes = passes + [((wzq[b][0][:], wzq[b][1][:]), zq[b, q]) for b in range(2)]
+                passes = [((wk_w[:, b], wk_s[:, b]), aq[b][q]) for b in range(2)]
+                passes = passes + [((wzq[b][0][:], wzq[b][1][:]), zq[b][q]) for b in range(2)]
                 for i, (weights, moving) in enumerate(passes):
                     for s in range(2):
                         cols = slice(P * (2 * k + s), P * (2 * k + s) + P)
                         nc.tensor.matmul_mx(out=bank[:, s, :], lhsT=weights[0][:, cols].bitcast(FP8X4), lhsT_scale=weights[1][:, cols],
-                                            rhs=moving[0][:].bitcast(FP8X4), rhs_scale=moving[1][:],
+                                            rhs=moving[0].bitcast(FP8X4), rhs_scale=moving[1],
                                             start=(i == 0 and s == 0), stop=(i == 3 and s == 1))
                 staged = ring.tile([P, 2, QW], F32, name="staged", bufs=4)
-                if k == 0:
+                if k == 0 and q == 3:
                     nc.vector.tensor_copy(staged[:], bank[:])
                 else:
                     nc.scalar.copy(staged[:], bank[:])
                 nc.sync.dma_start(
                     out=out[2 * P * k : 2 * P * k + 2 * P, QW * q : QW * q + QW].rearrange("(s p) j -> p s j", s=2), in_=staged[:])
 
-        diffs = []
-        for q in range(4):
-            a_bf = ring.tile([P, QW, 4], BF16, name="a_bf", bufs=4, align_bytes=64)
-            diffs.extend(machine(0, 2 * q + h, a_bf) for h in range(2))
-            aq[0, q] = quantize_tile(a_bf, "a0%d" % q)
-        for t in range(4):
-            place(1, t, grouped1)
-        for q in range(4):
-            z_bf = ring.tile([P, QW, 4], BF16, name="z_bf", bufs=4, align_bytes=64)
-            for h in range(2):
-                square(2 * q + h, diffs[2 * q + h], z_bf)
-            zq[0, q] = quantize_tile(z_bf, "z0%d" % q)
-        wzq = [quantize_wz(b) for b in range(2)]
+        aq, zq = [[], []], [[], []]
 
+        def interleaved(name):
+            return ring.tile([P, 2 * QW, 4], BF16, name=name, bufs=4, align_bytes=64)
+
+        diff0 = [held([P, 4, 2 * QW], F32, "diff0%d" % h, "slot_f%d" % h) for h in range(2)]
+        a_bf = [[interleaved("a_bf") for h in range(2)] for b in range(2)]
+        for c in range(8):
+            bank = machine(0, c, a_bf[0][c // 4])
+            col = CH * (c % 4)
+            for t in range(4):
+                subtract(0, t, diff0[c // 4][:, t, col : col + CH], bank[:, t, :], slice(CH * c, CH * c + CH))
+            if c == 3:
+                aq[0].extend(quantize_tokens(a_bf[0][0][:], 2 * QW, "a00"))
+        for t in range(3):
+            place(1, t, wbq1)
+
+        kept = held([P, 2, 4, QW], F32, "kept", "slot_b")
+        for c in range(4):
+            bank = machine(1, c, a_bf[1][0])
+            nc.scalar.copy(kept[:, c // 2, :, CH * (c % 2) : CH * (c % 2) + CH], bank[:])
+        aq[1].extend(quantize_tokens(a_bf[1][0][:], 2 * QW, "a10"))
+        banks = [machine(1, c, a_bf[1][1]) for c in range(4, 8)]
+        z_bf0 = [interleaved("z_bf") for h in range(2)]
+        square(z_bf0[0][:], diff0[0][:])
+        zq[0].extend(quantize_tokens(z_bf0[0][:], 2 * QW, "z00"))
+        place(1, 3, wbq1)
+        square(z_bf0[1][:], diff0[1][:])
+
+        diff1 = [held([P, 2, 4, QW], F32, "diff1%d" % h, "slot_f%d" % h) for h in range(2)]
+        late = held([P, 3, 2 * QW], U32, "late", "slot_g")
         for q in range(4):
-            a_bf = ring.tile([P, QW, 4], BF16, name="a_bf", bufs=4, align_bytes=64)
-            pair = [machine(1, 2 * q + h, a_bf) for h in range(2)]
-            aq[1, q] = quantize_tile(a_bf, "a1%d" % q)
-            z_bf = ring.tile([P, QW, 4], BF16, name="z_bf", bufs=4, align_bytes=64)
-            for h in range(2):
-                square(2 * q + h, pair[h], z_bf)
-            zq[1, q] = quantize_tile(z_bf, "z1%d" % q)
+            for t in range(4):
+                if q < 2:
+                    subtract(1, t, diff1[q // 2][:, q % 2, t, :], kept[:, q, t, :], slice(QW * q, QW * q + QW))
+            for c in range(2 * q, 2 * q + 2):
+                for t in range(4):
+                    if q >= 2:
+                        col = CH * (c % 2)
+                        subtract(1, t, diff1[q // 2][:, q % 2, t, col : col + CH], banks[c - 4][:, t, :], slice(CH * c, CH * c + CH))
+            z_bf = interleaved("z_bf")
+            square(z_bf[:, 0:QW, :], diff1[q // 2][:, q % 2])
+            zq[1].extend(quantize_tokens(z_bf[:, 0:QW, :], QW, "z1%d" % q))
+            if q == 1:
+                aq[0].extend(quantize_tokens(a_bf[0][1][:], 2 * QW, "a01", late[:, 0]))
+                aq[1].extend(quantize_tokens(a_bf[1][1][:], 2 * QW, "a11", late[:, 1]))
+                zq[0].extend(quantize_tokens(z_bf0[1][:], 2 * QW, "z01", late[:, 2]))
             if q > 0:
-                read_out(q - 1, wzq)
-        read_out(3, wzq)
+                read_out(q - 1)
+        read_out(3)

@@ -20,6 +20,10 @@ P = 128
 CH = 128
 QW = 256
 A_BANKS = 6
+PIECES = ((0, 256, 2), (256, 256, 2), (512, 256, 2), (768, 128, 4), (896, 128, 2))
+CAST_SPLIT = 40
+WGS_CUTS = (0, 1, 2, 4)
+QUADRANTS = (0, 2, 1, 3)
 
 
 def tile_list_ballot_audit_disagreement_kernel(
@@ -46,21 +50,22 @@ def tile_list_ballot_audit_disagreement_kernel(
         tab_s = held([P, T], U8, "tab_s")
         wa_raw = held([P, 2, H], U16, "wa_raw", "slot_d")
         wa_w = held([P, 2, H], U16, "wa_w")
-        wa_sraw = held([P, H], U8, "wa_sraw")
+        wa_sraw = held([P, H], U8, "wa_sraw", "slot_i")
         wa_s = [held([P, H], U8, "wa_s%d" % a) for a in range(2)]
-        wk_s = held([P, 2, N], U8, "wk_s")
-        wgs_t = [held([P, 2, PL], F32, "wgs_t0")]
+        wgs_t = [held([P, 1, PL], F32, "wgs_t%d" % h) for h in range(2)]
         pages = [held([P, S], F32, "page%d" % t) for t in range(4)]
         v_w = [held([P, S], U32, "v_w%d" % a) for a in range(2)]
+        v_rows = held([P, S], U8, "v_rows")
         v_s = [held([P, S], U8, "v_s%d" % a) for a in range(2)]
         v2_w = held([P, PL], U32, "v2_w")
         v2_s = held([P, PL], U8, "v2_s")
         gz_t = held([P, 8], F32, "gz_t")
         gb_t = held([P, 8], F32, "gb_t")
 
+        nc.gpsimd.memset(tab2_s[:].bitcast(I32), 0)
         nc.gpsimd.memset(tab_s[:].bitcast(I32), 0)
         nc.gpsimd.memset(wa_sraw[:].bitcast(I32), 0)
-        nc.gpsimd.memset(wk_s[:].bitcast(I32), 0)
+        nc.gpsimd.memset(v_s[0][:].bitcast(I32), 0)
         nc.gpsimd.memset(v_s[1][:].bitcast(I32), 0)
         nc.gpsimd.memset(wa_s[1][:].bitcast(I32), 0)
         for t in range(4):
@@ -69,9 +74,8 @@ def tile_list_ballot_audit_disagreement_kernel(
         nc.sync.dma_start(out=gz_t[:].rearrange("p (b t) -> p b t", b=2), in_=gz.rearrange("(b p t) -> p b t", b=2, t=4))
         nc.sync.dma_start(out=gb_t[:].rearrange("p (b t) -> p b t", b=2), in_=gb.rearrange("(b p t) -> p b t", b=2, t=4))
         nc.sync.dma_start(offs2_t[:], offs2)
-        for q in range(4):
-            rows = tab2_scales[0, 4 * q : 4 * q + 4, :].bitcast(I32).unsqueeze(0).to_broadcast([8, 4, TB // 4])
-            nc.sync.dma_start(out=tab2_s[32 * q : 32 * q + 32, :].bitcast(I32), in_=rows)
+        for q in QUADRANTS:
+            nc.sync.dma_start(out=tab2_s[32 * q : 32 * q + 4, :].bitcast(I32), in_=tab2_scales[0, 4 * q : 4 * q + 4, :].bitcast(I32))
         nc.sync.dma_start(out=tab2_w[:].bitcast(I32), in_=tab2_words[0].rearrange("p t i -> p (t i)").bitcast(I32))
 
         def load_rows(src, name, tag):
@@ -80,8 +84,8 @@ def tile_list_ballot_audit_disagreement_kernel(
             return raw
 
         def load_wgs(h):
-            rows = wgs.rearrange("(q t) c -> q t c", t=4)[:, 2 * h : 2 * h + 2, :]
-            for q in range(4):
+            rows = wgs.rearrange("(q t) c -> q t c", t=4)[:, WGS_CUTS[h] : WGS_CUTS[h + 1], :]
+            for q in QUADRANTS:
                 nc.sync.dma_start(out=wgs_t[h][32 * q : 32 * q + 32, :, :], in_=rows)
 
         def load_table(a):
@@ -100,15 +104,15 @@ def tile_list_ballot_audit_disagreement_kernel(
             for q in range(4):
                 nc.sync.dma_start(out=planes[1][32 * q : 32 * q + 4, :].bitcast(I32), in_=planes[0][32 * q + 4 : 32 * q + 8, :].bitcast(I32))
 
+        nc.sync.dma_start(offs_t[:], offs)
+        nc.sync.dma_start(out=tab_s[0:P:4, :].bitcast(I32), in_=tab_scales.rearrange("a q t -> (a q) t").bitcast(I32))
+        load_wgs(0)
         wb_raw = [load_rows(wb[:, 0:512], "wb_raw0", "slot_e")]
         nc.sync.dma_start(pos_t[:], pos1)
-        load_wgs(0)
+        load_wgs(1)
         load_table(0)
-        nc.sync.dma_start(offs_t[:], offs)
-        load_packed(tab_s, tab_scales)
         nc.sync.dma_start(out=wa_raw[:].bitcast(I32), in_=wa_words.rearrange("a p c -> p a c").bitcast(I32))
         load_packed(wa_sraw, wa_scales)
-        load_planes(wk_s, wk_scales)
 
         def small(name):
             return held([P, 8], F32, name)
@@ -130,9 +134,8 @@ def tile_list_ballot_audit_disagreement_kernel(
 
         nc.vector.tensor_copy(v2_w[:], tab2_w[:].indirect(offs2_t[:]))
         nc.vector.tensor_copy(v2_s[:], tab2_s[:].indirect(offs2_t[:]))
-        wz_raw = held([P, 2, 4, N], F32, "wz_raw", "slot_a")
-        for b in range(2):
-            nc.sync.dma_start(out=wz_raw[:, b], in_=wz[512 * b : 512 * b + 512, :].rearrange("(p j) c -> p j c", j=4))
+        nc.vector.tensor_copy(v_rows[:], tab_s[:].indirect(offs_t[:]))
+        wz_raw = [load_rows(wz[0:512, :], "wz_raw0", "slot_a")]
         tab_w.append(held([P, T], U32, "tab_w1", "slot_b"))
         load_table(1)
 
@@ -148,8 +151,8 @@ def tile_list_ballot_audit_disagreement_kernel(
             dst = grouped[:].rearrange("p t m j -> p m j t")
             src = wb_raw[b][:].rearrange("p j (m t) -> p m j t", t=4)
             if b == 0:
-                nc.vector.tensor_copy(dst[:, 0:64], src[:, 0:64])
-                nc.scalar.copy(dst[:, 64:128], src[:, 64:128])
+                nc.vector.tensor_copy(dst[:, 0:CAST_SPLIT], src[:, 0:CAST_SPLIT])
+                nc.scalar.copy(dst[:, CAST_SPLIT:P], src[:, CAST_SPLIT:P])
             else:
                 nc.scalar.copy(dst, src)
             return grouped
@@ -165,9 +168,11 @@ def tile_list_ballot_audit_disagreement_kernel(
                                 rhs=v2_w[:].bitcast(FP8X4), rhs_scale=v2_s[:], start=True, stop=True)
             if (b, t) == (1, 3):
                 weight = held([P, PL], F32, "weight_last", "slot_f0")
+            elif b == 0 and t >= 2:
+                weight = held([P, PL], F32, "weight0%d" % t, "slot_h%d" % t)
             else:
-                weight = ring.tile([P, PL], F32, name="weight", bufs=7)
-            nc.scalar.activation(weight[:], wgs_t[t // 2][:, t % 2, :], ACT.Copy, scale=root_gb[:, 4 * b + t : 4 * b + t + 1])
+                weight = ring.tile([P, PL], F32, name="weight", bufs=5)
+            nc.scalar.activation(weight[:], wgs_t[min(t, 2)][:, max(t - 2, 0), :], ACT.Copy, scale=root_gb[:, 4 * b + t : 4 * b + t + 1])
             if (b, t) == (1, 3):
                 hand = held([P, PL], F32, "hand_last", "slot_g")
             else:
@@ -176,15 +181,20 @@ def tile_list_ballot_audit_disagreement_kernel(
             nc.vector.tensor_tensor(pages[t][:].indirect(pos_t[:]), hand[:], weight[:], ALU.mult)
 
         grouped0 = cast_wb(0)
-        wgs_t.append(held([P, 2, PL], F32, "wgs_t1", "slot_e"))
-        load_wgs(1)
+        later = held([P, 6, PL], F32, "later", "slot_e")
+        wgs_t.append(later[:, 0:2])
+        load_wgs(2)
+        wz_raw.append(later[:, 2:6])
+        nc.sync.dma_start(out=wz_raw[1], in_=wz[512:1024, :].rearrange("(p j) c -> p j c", j=4))
         wbq0 = quantize_wb(grouped0, 0, 1, "wb00")
         place(0, 0, wbq0)
         wbq0 = wbq0 + quantize_wb(grouped0, 1, 2, "wb01") + quantize_wb(grouped0, 2, 4, "wb02")
         place(0, 1, wbq0)
 
-        nc.vector.tensor_copy(v_s[0][:], tab_s[:].indirect(offs_t[:]))
-        lift_second_plane(v_s)
+        for a in range(2):
+            for q in range(4):
+                first = 64 * a + 16 * q
+                nc.sync.dma_start(out=v_s[a][32 * q : 32 * q + 4, :].bitcast(I32), in_=v_rows[first : first + 16 : 4, :].bitcast(I32))
         nc.vector.tensor_copy(wa_s[0][:].rearrange("p (b t m) -> p b m t", b=2, t=4), wa_sraw[:].rearrange("p (b m t) -> p b m t", b=2, t=4))
         lift_second_plane(wa_s)
         nc.vector.tensor_copy(v_w[0][:], tab_w[0][:].indirect(offs_t[:]))
@@ -193,19 +203,25 @@ def tile_list_ballot_audit_disagreement_kernel(
                               wa_raw[:].rearrange("p a (b m t) -> p (a b) m t", b=2, t=4))
         wk_w = held([P, 2, N], U32, "wk_w", "slot_d")
         nc.sync.dma_start(out=wk_w[:].bitcast(I32), in_=wk_words.rearrange("a p c i -> p a (c i)").bitcast(I32))
+        wk_s = held([P, 2, N], U8, "wk_s", "slot_i")
+        nc.gpsimd.memset(wk_s[:].bitcast(I32), 0)
+        load_planes(wk_s, wk_scales)
         nc.vector.tensor_copy(v_w[1][:], tab_w[1][:].indirect(offs_t[:]))
 
         def quantize_wz(b):
             signed = ring.tile([P, 4, N], BF16, name="signed", bufs=1)
             for j in range(4):
-                nc.scalar.activation(signed[:, j, :], wz_raw[:, b, j, :], ACT.Copy, scale=sign[:, 4 * b + j : 4 * b + j + 1])
+                nc.scalar.activation(signed[:, j, :], wz_raw[b][:, j, :], ACT.Copy, scale=sign[:, 4 * b + j : 4 * b + j + 1])
             grouped = ring.tile([P, 4, P, 4], BF16, name="wz_bf%d" % b, tag="grouped", bufs=3, align_bytes=64)
             nc.scalar.copy(grouped[:].rearrange("p s (c i) j -> p (s c) j i", i=4), signed[:].rearrange("p j (c i) -> p c j i", i=4))
-            return quantize(grouped[:].rearrange("p s m j -> p (s m j)"), N, "wz%d" % b)
+            return grouped
 
-        wzq = [quantize_wz(b) for b in range(2)]
+        wz_bf = [quantize_wz(0)]
         place(0, 2, wbq0)
         place(0, 3, wbq0)
+        wz_bf.append(quantize_wz(1))
+        wzq = [quantize(wz_bf[b][:].rearrange("p s m j -> p (s m j)"), N, "wz%d" % b, held([P, N], U32, "wz%d_w" % b, "slot_h%d" % (2 + b)))
+               for b in range(2)]
         wbq1 = quantize_wb(cast_wb(1), 0, 4, "wb1")
 
         def machine(b, c, a_bf):
@@ -229,32 +245,34 @@ def tile_list_ballot_audit_disagreement_kernel(
                                  ACT.Square, scale=0.5)
 
         def quantize_tokens(src, width, name, codes=None):
-            codes, scales = quantize(src.rearrange("p c t -> p (c t)"), width, name, codes)
-            return [(codes[:, QW * i : QW * i + QW], scales[:, QW * i : QW * i + QW]) for i in range(width // QW)]
+            return quantize(src.rearrange("p c t -> p (c t)"), width, name, codes)
 
-        def read_out(q):
-            for k in range(2):
-                if q == 0:
-                    bank = psum.tile([P, 2, QW], F32, name="o_bank", tag="bo", bufs=2)
+        def read_out(first, width, z_last, per_bank):
+            half, col = divmod(first, 2 * QW)
+            tokens = slice(col, col + width)
+            for n0 in range(0, 4, per_bank):
+                if first == 0:
+                    bank = psum.tile([P, per_bank, width], F32, name="o_bank", tag="bo", bufs=2)
                 else:
-                    bank = psum.tile([P, 2, QW], F32, name="o_bank", tag="a", bufs=A_BANKS)
-                passes = [((wk_w[:, b], wk_s[:, b]), aq[b][q]) for b in range(2)]
-                passes = passes + [((wzq[b][0][:], wzq[b][1][:]), zq[b][q]) for b in range(2)]
-                for i, (weights, moving) in enumerate(passes):
-                    for s in range(2):
-                        cols = slice(P * (2 * k + s), P * (2 * k + s) + P)
+                    bank = psum.tile([P, per_bank, width], F32, name="o_bank", tag="a", bufs=A_BANKS)
+                passes = [((wk_w[:, b], wk_s[:, b]), aq[b][half], tokens) for b in range(2)]
+                passes.append((wzq[0], zq0[half], tokens))
+                passes.append((wzq[1], z_last, slice(0, width)))
+                for i, (weights, moving, window) in enumerate(passes):
+                    for s in range(per_bank):
+                        cols = slice(P * (n0 + s), P * (n0 + s) + P)
                         nc.tensor.matmul_mx(out=bank[:, s, :], lhsT=weights[0][:, cols].bitcast(FP8X4), lhsT_scale=weights[1][:, cols],
-                                            rhs=moving[0].bitcast(FP8X4), rhs_scale=moving[1],
-                                            start=(i == 0 and s == 0), stop=(i == 3 and s == 1))
-                staged = ring.tile([P, 2, QW], F32, name="staged", bufs=4)
-                if k == 0 and q == 3:
+                                            rhs=moving[0][:, window].bitcast(FP8X4), rhs_scale=moving[1][:, window],
+                                            start=(i == 0 and s == 0), stop=(i == 3 and s == per_bank - 1))
+                staged = ring.tile([P, per_bank, width], F32, name="staged", bufs=8)
+                if n0 == 0 and first + width == S:
                     nc.vector.tensor_copy(staged[:], bank[:])
                 else:
                     nc.scalar.copy(staged[:], bank[:])
                 nc.sync.dma_start(
-                    out=out[2 * P * k : 2 * P * k + 2 * P, QW * q : QW * q + QW].rearrange("(s p) j -> p s j", s=2), in_=staged[:])
+                    out=out[P * n0 : P * (n0 + per_bank), first : first + width].rearrange("(s p) j -> p s j", s=per_bank), in_=staged[:])
 
-        aq, zq = [[], []], [[], []]
+        aq, zq0 = [[], []], []
 
         def interleaved(name):
             return ring.tile([P, 2 * QW, 4], BF16, name=name, bufs=4, align_bytes=64)
@@ -267,7 +285,7 @@ def tile_list_ballot_audit_disagreement_kernel(
             for t in range(4):
                 subtract(0, t, diff0[c // 4][:, t, col : col + CH], bank[:, t, :], slice(CH * c, CH * c + CH))
             if c == 3:
-                aq[0].extend(quantize_tokens(a_bf[0][0][:], 2 * QW, "a00"))
+                aq[0].append(quantize_tokens(a_bf[0][0][:], 2 * QW, "a00"))
         for t in range(3):
             place(1, t, wbq1)
 
@@ -275,32 +293,35 @@ def tile_list_ballot_audit_disagreement_kernel(
         for c in range(4):
             bank = machine(1, c, a_bf[1][0])
             nc.scalar.copy(kept[:, c // 2, :, CH * (c % 2) : CH * (c % 2) + CH], bank[:])
-        aq[1].extend(quantize_tokens(a_bf[1][0][:], 2 * QW, "a10"))
+        aq[1].append(quantize_tokens(a_bf[1][0][:], 2 * QW, "a10"))
         banks = [machine(1, c, a_bf[1][1]) for c in range(4, 8)]
         z_bf0 = [interleaved("z_bf") for h in range(2)]
         square(z_bf0[0][:], diff0[0][:])
-        zq[0].extend(quantize_tokens(z_bf0[0][:], 2 * QW, "z00"))
+        zq0.append(quantize_tokens(z_bf0[0][:], 2 * QW, "z00"))
         place(1, 3, wbq1)
         square(z_bf0[1][:], diff0[1][:])
 
-        diff1 = [held([P, 2, 4, QW], F32, "diff1%d" % h, "slot_f%d" % h) for h in range(2)]
+        diff1 = [held([P, 4, 2 * QW], F32, "diff1%d" % h, "slot_f%d" % h) for h in range(2)]
         late = held([P, 3, 2 * QW], U32, "late", "slot_g")
-        for q in range(4):
-            for t in range(4):
-                if q < 2:
-                    subtract(1, t, diff1[q // 2][:, q % 2, t, :], kept[:, q, t, :], slice(QW * q, QW * q + QW))
-            for c in range(2 * q, 2 * q + 2):
+        done = []
+        for first, width, per_bank in PIECES:
+            half, col = divmod(first, 2 * QW)
+            diff = diff1[half][:, :, col : col + width]
+            if half == 0:
                 for t in range(4):
-                    if q >= 2:
-                        col = CH * (c % 2)
-                        subtract(1, t, diff1[q // 2][:, q % 2, t, col : col + CH], banks[c - 4][:, t, :], slice(CH * c, CH * c + CH))
+                    subtract(1, t, diff[:, t, :], kept[:, first // QW, t, :], slice(first, first + width))
+            else:
+                for c in range(first // CH, (first + width) // CH):
+                    for t in range(4):
+                        subtract(1, t, diff1[1][:, t, CH * (c - 4) : CH * (c - 3)], banks[c - 4][:, t, :], slice(CH * c, CH * c + CH))
             z_bf = interleaved("z_bf")
-            square(z_bf[:, 0:QW, :], diff1[q // 2][:, q % 2])
-            zq[1].extend(quantize_tokens(z_bf[:, 0:QW, :], QW, "z1%d" % q))
-            if q == 1:
-                aq[0].extend(quantize_tokens(a_bf[0][1][:], 2 * QW, "a01", late[:, 0]))
-                aq[1].extend(quantize_tokens(a_bf[1][1][:], 2 * QW, "a11", late[:, 1]))
-                zq[0].extend(quantize_tokens(z_bf0[1][:], 2 * QW, "z01", late[:, 2]))
-            if q > 0:
-                read_out(q - 1)
-        read_out(3)
+            square(z_bf[:, 0:width, :], diff)
+            z_last = quantize_tokens(z_bf[:, 0:width, :], width, "z1_%d" % first)
+            if first == QW:
+                aq[0].append(quantize_tokens(a_bf[0][1][:], 2 * QW, "a01", late[:, 0]))
+                aq[1].append(quantize_tokens(a_bf[1][1][:], 2 * QW, "a11", late[:, 1]))
+                zq0.append(quantize_tokens(z_bf0[1][:], 2 * QW, "z01", late[:, 2]))
+            if done:
+                read_out(*done[-1])
+            done.append((first, width, z_last, per_bank))
+        read_out(*done[-1])

from contextlib import ExitStack

import concourse.mybir as mybir

K, KB, H, N, T, S, TB, PL = 1024, 512, 1024, 512, 4096, 1024, 2048, 512
FLOPS = 2 * K * H * S + 2 * KB * H * PL + 2 * 2 * H * N * S

F32 = mybir.dt.float32
BF16 = mybir.dt.bfloat16
I32 = mybir.dt.int32
U32 = mybir.dt.uint32
U16 = mybir.dt.uint16
U8 = mybir.dt.uint8
FP8X4 = mybir.dt.float8_e4m3fn_x4
FP4X4 = mybir.dt.float4_e2m1fn_x4
ALU = mybir.AluOpType
ACT = mybir.ActivationFunctionType

P = 128
CH = 128
QW = 256
A_BANKS = 6
PIECES = ((0, 256, 2), (256, 256, 2), (512, 256, 2), (768, 128, 4), (896, 128, 2))
CAST_SPLIT = 40
WGS_CUTS = (0, 1, 2, 4)
QUADRANTS = (0, 2, 1, 3)


def tile_list_ballot_audit_disagreement_kernel(
    tc, tab_words, tab_scales, tab2_words, tab2_scales, offs, offs2, pos1,
    wa_words, wa_scales, wb, gb, wgs, gz, wz, wk_words, wk_scales, out,
):
    nc = tc.nc
    with ExitStack() as ctx:
        lists = ctx.enter_context(tc.tile_pool(name="lists", bufs=1))
        keep = ctx.enter_context(tc.tile_pool(name="keep", bufs=1))
        ring = ctx.enter_context(tc.tile_pool(name="ring", bufs=2))
        psum = ctx.enter_context(tc.psum_pool(name="psum", bufs=1))

        offs_t = lists.tile([P, S // 16], U16, name="offs_t")
        offs2_t = lists.tile([P, PL // 16], U16, name="offs2_t")
        pos_t = lists.tile([P, PL // 16], U16, name="pos_t")

        def held(shape, dtype, name, tag=""):
            return keep.tile(shape, dtype, name=name, tag=tag, align_bytes=64)

        tab2_w = held([P, TB], U32, "tab2_w", "slot_a")
        tab2_s = held([P, TB], U8, "tab2_s", "slot_b")
        tab_w = [held([P, T], U32, "tab_w0", "slot_c")]
        tab_s = held([P, T], U8, "tab_s")
        wa_raw = held([P, 2, H], U16, "wa_raw", "slot_d")
        wa_w = held([P, 2, H], U16, "wa_w")
        wa_sraw = held([P, H], U8, "wa_sraw", "slot_i")
        wa_s = [held([P, H], U8, "wa_s%d" % a) for a in range(2)]
        wgs_t = [held([P, 1, PL], F32, "wgs_t%d" % h) for h in range(2)]
        pages = [held([P, S], F32, "page%d" % t) for t in range(4)]
        v_w = [held([P, S], U32, "v_w%d" % a) for a in range(2)]
        v_rows = held([P, S], U8, "v_rows")
        v_s = [held([P, S], U8, "v_s%d" % a) for a in range(2)]
        v2_w = held([P, PL], U32, "v2_w")
        v2_s = held([P, PL], U8, "v2_s")
        gz_t = held([P, 8], F32, "gz_t")
        gb_t = held([P, 8], F32, "gb_t")

        nc.gpsimd.memset(tab2_s[:].bitcast(I32), 0)
        nc.gpsimd.memset(tab_s[:].bitcast(I32), 0)
        nc.gpsimd.memset(wa_sraw[:].bitcast(I32), 0)
        nc.gpsimd.memset(v_s[0][:].bitcast(I32), 0)
        nc.gpsimd.memset(v_s[1][:].bitcast(I32), 0)
        nc.gpsimd.memset(wa_s[1][:].bitcast(I32), 0)
        for t in range(4):
            nc.vector.memset(pages[t][:], 0.0)

        nc.sync.dma_start(out=gz_t[:].rearrange("p (b t) -> p b t", b=2), in_=gz.rearrange("(b p t) -> p b t", b=2, t=4))
        nc.sync.dma_start(out=gb_t[:].rearrange("p (b t) -> p b t", b=2), in_=gb.rearrange("(b p t) -> p b t", b=2, t=4))
        nc.sync.dma_start(offs2_t[:], offs2)
        for q in QUADRANTS:
            nc.sync.dma_start(out=tab2_s[32 * q : 32 * q + 4, :].bitcast(I32), in_=tab2_scales[0, 4 * q : 4 * q + 4, :].bitcast(I32))
        nc.sync.dma_start(out=tab2_w[:].bitcast(I32), in_=tab2_words[0].rearrange("p t i -> p (t i)").bitcast(I32))

        def load_rows(src, name, tag):
            raw = held([P, 4, 512], F32, name, tag)
            nc.sync.dma_start(out=raw[:], in_=src.rearrange("(p j) c -> p j c", j=4))
            return raw

        def load_wgs(h):
            rows = wgs.rearrange("(q t) c -> q t c", t=4)[:, WGS_CUTS[h] : WGS_CUTS[h + 1], :]
            for q in QUADRANTS:
                nc.sync.dma_start(out=wgs_t[h][32 * q : 32 * q + 32, :, :], in_=rows)

        def load_table(a):
            nc.sync.dma_start(out=tab_w[a][:].bitcast(I32), in_=tab_words[a].rearrange("p t i -> p (t i)").bitcast(I32))

        def load_planes(dst, src):
            rows = src.rearrange("a (q r) c -> r q a c", r=4)
            for r in range(4):
                nc.sync.dma_start(out=dst[r:P:32, :, :].bitcast(I32), in_=rows[r].bitcast(I32))

        def load_packed(dst, src):
            for q in range(4):
                nc.sync.dma_start(out=dst[32 * q : 32 * q + 8, :].bitcast(I32), in_=src[:, 4 * q : 4 * q + 4, :].bitcast(I32))

        def lift_second_plane(planes):
            for q in range(4):
                nc.sync.dma_start(out=planes[1][32 * q : 32 * q + 4, :].bitcast(I32), in_=planes[0][32 * q + 4 : 32 * q + 8, :].bitcast(I32))

        nc.sync.dma_start(offs_t[:], offs)
        nc.sync.dma_start(out=tab_s[0:P:4, :].bitcast(I32), in_=tab_scales.rearrange("a q t -> (a q) t").bitcast(I32))
        load_wgs(0)
        wb_raw = [load_rows(wb[:, 0:512], "wb_raw0", "slot_e")]
        nc.sync.dma_start(pos_t[:], pos1)
        load_wgs(1)
        load_table(0)
        nc.sync.dma_start(out=wa_raw[:].bitcast(I32), in_=wa_words.rearrange("a p c -> p a c").bitcast(I32))
        load_packed(wa_sraw, wa_scales)

        def small(name):
            return held([P, 8], F32, name)

        twice, sign, mag, safe = small("twice"), small("sign"), small("mag"), small("safe")
        guess, inverse, ratio = small("guess"), small("inverse"), small("ratio")
        root, root_gb = small("root"), small("root_gb")
        nc.vector.scalar_tensor_tensor(mag[:], gz_t[:], -1.0, gz_t[:], ALU.mult, ALU.max)
        nc.vector.tensor_scalar(safe[:], mag[:], 1e-30, None, ALU.max)
        nc.scalar.activation(guess[:], safe[:], ACT.Sqrt)
        warm = held([P, 8], F32, "warm")
        nc.scalar.activation(warm[:], guess[:], ACT.Tanh)
        nc.vector.reciprocal(inverse[:], guess[:])
        nc.vector.tensor_tensor(ratio[:], mag[:], inverse[:], ALU.mult)
        nc.vector.tensor_tensor(root[:], ratio[:], guess[:], ALU.add)
        nc.vector.tensor_tensor(root_gb[:], root[:], gb_t[:], ALU.mult)
        nc.vector.tensor_scalar(twice[:], gz_t[:], 0.0, 2.0, ALU.is_ge, ALU.mult)
        nc.vector.tensor_scalar(sign[:], twice[:], -1.0, None, ALU.add)

        nc.vector.tensor_copy(v2_w[:], tab2_w[:].indirect(offs2_t[:]))
        nc.vector.tensor_copy(v2_s[:], tab2_s[:].indirect(offs2_t[:]))
        nc.vector.tensor_copy(v_rows[:], tab_s[:].indirect(offs_t[:]))
        wz_raw = [load_rows(wz[0:512, :], "wz_raw0", "slot_a")]
        tab_w.append(held([P, T], U32, "tab_w1", "slot_b"))
        load_table(1)

        def quantize(src, width, name, codes=None):
            if codes is None:
                codes = held([P, width], U32, name + "_w")
            scales = held([P, width], U8, name + "_s")
            nc.vector.quantize_mx(out=codes[:].bitcast(FP8X4), scales=scales[:], in_=src)
            return codes, scales

        def cast_wb(b):
            grouped = ring.tile([P, 4, P, 4], BF16, name="wb_bf%d" % b, tag="grouped", bufs=3, align_bytes=64)
            dst = grouped[:].rearrange("p t m j -> p m j t")
            src = wb_raw[b][:].rearrange("p j (m t) -> p m j t", t=4)
            if b == 0:
                nc.vector.tensor_copy(dst[:, 0:CAST_SPLIT], src[:, 0:CAST_SPLIT])
                nc.scalar.copy(dst[:, CAST_SPLIT:P], src[:, CAST_SPLIT:P])
            else:
                nc.scalar.copy(dst, src)
            return grouped

        def quantize_wb(grouped, t0, t1, name):
            codes, scales = quantize(grouped[:, t0:t1].rearrange("p t m j -> p (t m j)"), P * (t1 - t0), name)
            return [(codes[:, P * i : P * i + P], scales[:, P * i : P * i + P]) for i in range(t1 - t0)]

        def place(b, t, weights):
            codes, scales = weights[t]
            bank = psum.tile([P, PL], F32, name="b_bank", tag="bo", bufs=2)
            nc.tensor.matmul_mx(out=bank[:], lhsT=codes.bitcast(FP8X4), lhsT_scale=scales,
                                rhs=v2_w[:].bitcast(FP8X4), rhs_scale=v2_s[:], start=True, stop=True)
            if (b, t) == (1, 3):
                weight = held([P, PL], F32, "weight_last", "slot_f0")
            elif b == 0 and t >= 2:
                weight = held([P, PL], F32, "weight0%d" % t, "slot_h%d" % t)
            else:
                weight = ring.tile([P, PL], F32, name="weight", bufs=5)
            nc.scalar.activation(weight[:], wgs_t[min(t, 2)][:, max(t - 2, 0), :], ACT.Copy, scale=root_gb[:, 4 * b + t : 4 * b + t + 1])
            if (b, t) == (1, 3):
                hand = held([P, PL], F32, "hand_last", "slot_g")
            else:
                hand = ring.tile([P, PL], F32, name="hand", bufs=7)
            nc.scalar.activation(hand[:], bank[:], ACT.Tanh)
            nc.vector.tensor_tensor(pages[t][:].indirect(pos_t[:]), hand[:], weight[:], ALU.mult)

        grouped0 = cast_wb(0)
        later = held([P, 6, PL], F32, "later", "slot_e")
        wgs_t.append(later[:, 0:2])
        load_wgs(2)
        wz_raw.append(later[:, 2:6])
        nc.sync.dma_start(out=wz_raw[1], in_=wz[512:1024, :].rearrange("(p j) c -> p j c", j=4))
        wbq0 = quantize_wb(grouped0, 0, 1, "wb00")
        place(0, 0, wbq0)
        wbq0 = wbq0 + quantize_wb(grouped0, 1, 2, "wb01") + quantize_wb(grouped0, 2, 4, "wb02")
        place(0, 1, wbq0)

        for a in range(2):
            for q in range(4):
                first = 64 * a + 16 * q
                nc.sync.dma_start(out=v_s[a][32 * q : 32 * q + 4, :].bitcast(I32), in_=v_rows[first : first + 16 : 4, :].bitcast(I32))
        nc.vector.tensor_copy(wa_s[0][:].rearrange("p (b t m) -> p b m t", b=2, t=4), wa_sraw[:].rearrange("p (b m t) -> p b m t", b=2, t=4))
        lift_second_plane(wa_s)
        nc.vector.tensor_copy(v_w[0][:], tab_w[0][:].indirect(offs_t[:]))
        wb_raw.append(load_rows(wb[:, 512:1024], "wb_raw1", "slot_c"))
        nc.vector.tensor_copy(wa_w[:].rearrange("p a (b t m) -> p (a b) m t", b=2, t=4),
                              wa_raw[:].rearrange("p a (b m t) -> p (a b) m t", b=2, t=4))
        wk_w = held([P, 2, N], U32, "wk_w", "slot_d")
        nc.sync.dma_start(out=wk_w[:].bitcast(I32), in_=wk_words.rearrange("a p c i -> p a (c i)").bitcast(I32))
        wk_s = held([P, 2, N], U8, "wk_s", "slot_i")
        nc.gpsimd.memset(wk_s[:].bitcast(I32), 0)
        load_planes(wk_s, wk_scales)
        nc.vector.tensor_copy(v_w[1][:], tab_w[1][:].indirect(offs_t[:]))

        def quantize_wz(b):
            signed = ring.tile([P, 4, N], BF16, name="signed", bufs=1)
            for j in range(4):
                nc.scalar.activation(signed[:, j, :], wz_raw[b][:, j, :], ACT.Copy, scale=sign[:, 4 * b + j : 4 * b + j + 1])
            grouped = ring.tile([P, 4, P, 4], BF16, name="wz_bf%d" % b, tag="grouped", bufs=3, align_bytes=64)
            nc.scalar.copy(grouped[:].rearrange("p s (c i) j -> p (s c) j i", i=4), signed[:].rearrange("p j (c i) -> p c j i", i=4))
            return grouped

        wz_bf = [quantize_wz(0)]
        place(0, 2, wbq0)
        place(0, 3, wbq0)
        wz_bf.append(quantize_wz(1))
        wzq = [quantize(wz_bf[b][:].rearrange("p s m j -> p (s m j)"), N, "wz%d" % b, held([P, N], U32, "wz%d_w" % b, "slot_h%d" % (2 + b)))
               for b in range(2)]
        wbq1 = quantize_wb(cast_wb(1), 0, 4, "wb1")

        def machine(b, c, a_bf):
            bank = psum.tile([P, 4, CH], F32, name="a_bank", tag="a", bufs=A_BANKS)
            cols = slice(CH * c, CH * c + CH)
            for a in range(2):
                for t in range(4):
                    rows = slice(512 * b + P * t, 512 * b + P * t + P)
                    nc.tensor.matmul_mx(out=bank[:, t, :], lhsT=wa_w[:, a, rows].bitcast(FP4X4), lhsT_scale=wa_s[a][:, rows],
                                        rhs=v_w[a][:, cols].bitcast(FP8X4), rhs_scale=v_s[a][:, cols],
                                        start=(a == 0 and t == 0), stop=(a == 1 and t == 3))
            part = c % 4
            nc.scalar.copy(a_bf[:, CH * part : CH * part + CH, :], bank[:].rearrange("p t c -> p c t"))
            return bank

        def subtract(b, t, dst, src, cols):
            nc.vector.scalar_tensor_tensor(dst, src, root[:, 4 * b + t : 4 * b + t + 1], pages[t][:, cols], ALU.mult, ALU.subtract)

        def square(dst, src):
            nc.scalar.activation(dst.rearrange("p (c i) t -> p c t i", i=4), src.rearrange("p t (c i) -> p c t i", i=4),
                                 ACT.Square, scale=0.5)

        def quantize_tokens(src, width, name, codes=None):
            return quantize(src.rearrange("p c t -> p (c t)"), width, name, codes)

        def read_out(first, width, z_last, per_bank):
            half, col = divmod(first, 2 * QW)
            tokens = slice(col, col + width)
            for n0 in range(0, 4, per_bank):
                if first == 0:
                    bank = psum.tile([P, per_bank, width], F32, name="o_bank", tag="bo", bufs=2)
                else:
                    bank = psum.tile([P, per_bank, width], F32, name="o_bank", tag="a", bufs=A_BANKS)
                passes = [((wk_w[:, b], wk_s[:, b]), aq[b][half], tokens) for b in range(2)]
                passes.append((wzq[0], zq0[half], tokens))
                passes.append((wzq[1], z_last, slice(0, width)))
                for i, (weights, moving, window) in enumerate(passes):
                    for s in range(per_bank):
                        cols = slice(P * (n0 + s), P * (n0 + s) + P)
                        nc.tensor.matmul_mx(out=bank[:, s, :], lhsT=weights[0][:, cols].bitcast(FP8X4), lhsT_scale=weights[1][:, cols],
                                            rhs=moving[0][:, window].bitcast(FP8X4), rhs_scale=moving[1][:, window],
                                            start=(i == 0 and s == 0), stop=(i == 3 and s == per_bank - 1))
                staged = ring.tile([P, per_bank, width], F32, name="staged", bufs=8)
                if n0 == 0 and first + width == S:
                    nc.vector.tensor_copy(staged[:], bank[:])
                else:
                    nc.scalar.copy(staged[:], bank[:])
                nc.sync.dma_start(
                    out=out[P * n0 : P * (n0 + per_bank), first : first + width].rearrange("(s p) j -> p s j", s=per_bank), in_=staged[:])

        aq, zq0 = [[], []], []

        def interleaved(name):
            return ring.tile([P, 2 * QW, 4], BF16, name=name, bufs=4, align_bytes=64)

        diff0 = [held([P, 4, 2 * QW], F32, "diff0%d" % h, "slot_f%d" % h) for h in range(2)]
        a_bf = [[interleaved("a_bf") for h in range(2)] for b in range(2)]
        for c in range(8):
            bank = machine(0, c, a_bf[0][c // 4])
            col = CH * (c % 4)
            for t in range(4):
                subtract(0, t, diff0[c // 4][:, t, col : col + CH], bank[:, t, :], slice(CH * c, CH * c + CH))
            if c == 3:
                aq[0].append(quantize_tokens(a_bf[0][0][:], 2 * QW, "a00"))
        for t in range(3):
            place(1, t, wbq1)

        kept = held([P, 2, 4, QW], F32, "kept", "slot_b")
        for c in range(4):
            bank = machine(1, c, a_bf[1][0])
            nc.scalar.copy(kept[:, c // 2, :, CH * (c % 2) : CH * (c % 2) + CH], bank[:])
        aq[1].append(quantize_tokens(a_bf[1][0][:], 2 * QW, "a10"))
        banks = [machine(1, c, a_bf[1][1]) for c in range(4, 8)]
        z_bf0 = [interleaved("z_bf") for h in range(2)]
        square(z_bf0[0][:], diff0[0][:])
        zq0.append(quantize_tokens(z_bf0[0][:], 2 * QW, "z00"))
        place(1, 3, wbq1)
        square(z_bf0[1][:], diff0[1][:])

        diff1 = [held([P, 4, 2 * QW], F32, "diff1%d" % h, "slot_f%d" % h) for h in range(2)]
        late = held([P, 3, 2 * QW], U32, "late", "slot_g")
        done = []
        for first, width, per_bank in PIECES:
            half, col = divmod(first, 2 * QW)
            diff = diff1[half][:, :, col : col + width]
            if half == 0:
                for t in range(4):
                    subtract(1, t, diff[:, t, :], kept[:, first // QW, t, :], slice(first, first + width))
            else:
                for c in range(first // CH, (first + width) // CH):
                    for t in range(4):
                        subtract(1, t, diff1[1][:, t, CH * (c - 4) : CH * (c - 3)], banks[c - 4][:, t, :], slice(CH * c, CH * c + CH))
            z_bf = interleaved("z_bf")
            square(z_bf[:, 0:width, :], diff)
            z_last = quantize_tokens(z_bf[:, 0:width, :], width, "z1_%d" % first)
            if first == QW:
                aq[0].append(quantize_tokens(a_bf[0][1][:], 2 * QW, "a01", late[:, 0]))
                aq[1].append(quantize_tokens(a_bf[1][1][:], 2 * QW, "a11", late[:, 1]))
                zq0.append(quantize_tokens(z_bf0[1][:], 2 * QW, "z01", late[:, 2]))
            if done:
                read_out(*done[-1])
            done.append((first, width, z_last, per_bank))
        read_out(*done[-1])
